import numpy as np
import ml_dtypes


def mxq(x, axis, fmt="e4m3"):
    dtype, down = {"e4m3": (ml_dtypes.float8_e4m3fn, 7), "e5m2": (ml_dtypes.float8_e5m2, 14)}[fmt]
    v = np.moveaxis(np.asarray(x, np.float32).astype(ml_dtypes.bfloat16).astype(np.float64), axis, -1)
    blocks = v.reshape(v.shape[:-1] + (-1, 32))
    amax = np.abs(blocks).max(-1, keepdims=True)
    byte = np.maximum(np.where(amax > 0, np.frexp(amax)[1] - 1 + 127, 0) - down, 1)
    scale = np.exp2(byte - 127.0)
    codes = (blocks / scale).astype(np.float32).astype(dtype).astype(np.float64)
    return np.moveaxis((codes * scale).reshape(v.shape), -1, axis)


WIDE = False


def mx_kscale(k):
    if not WIDE:
        return np.ones(k)
    levels = np.array([10, -10, 5, -5, 0])
    if k % 512:
        return np.exp2(np.random.permutation(np.resize(levels, k // 32))).repeat(32)
    a = np.empty((k // 512, 16))
    for p in range(k // 512):
        a[p, :8] = np.random.permutation(np.resize(levels, 8))
        for g in range(8):
            far = levels[np.abs(levels - a[p, g]) >= 10]
            a[p, g + 8] = far[np.random.randint(len(far))]
    return np.exp2(a.ravel()).repeat(32)


def f64(x):
    return np.asarray(x).astype(np.float64)


def striped8(idx):
    return np.asarray(idx).reshape(8, -1, 16).transpose(0, 2, 1).reshape(128, -1).astype(np.uint16)


def unstriped8(offs):
    return offs.reshape(8, 16, -1).transpose(0, 2, 1).reshape(8, -1).astype(np.int64)


def pick8(x, idx, run):
    r = np.arange(len(x))
    return x[r[:, None], idx[r % (8 * run) // run]]


E2M1 = np.array([0.0, 0.5, 1.0, 1.5, 2.0, 3.0, 4.0, 6.0, -0.0, -0.5, -1.0, -1.5, -2.0, -3.0, -4.0, -6.0])


def pack_weight(w, fmt):
    k, n = w.shape
    w = f64(np.asarray(w, np.float32).astype(ml_dtypes.bfloat16)).reshape(k // 32, 32, n)
    amax = np.abs(w).max(1)
    if fmt == "e4m3":
        byte = np.frexp(amax)[1] - 1 + 127 - 7
    else:
        mant, ex = np.frexp(amax / 6.0)
        byte = np.where(mant > 0.5, ex, ex - 1) + 127
    byte = np.clip(np.where(amax > 0, byte, 1), 1, 254)
    scaled = (w * np.exp2(127.0 - byte)[:, None, :]).reshape(k, n).astype(np.float32)
    by_word = np.ascontiguousarray(scaled.reshape(k // 512, 128, 4, n).transpose(0, 1, 3, 2))
    if fmt == "e4m3":
        words = by_word.astype(ml_dtypes.float8_e4m3fn).view(np.uint8)
    else:
        c = by_word.astype(ml_dtypes.float4_e2m1fn).view(np.uint8) & 0xF
        words = (c[..., 0::2] | (c[..., 1::2] << 4)).reshape(k // 512, 128, 2 * n)
    return np.ascontiguousarray(words), np.ascontiguousarray(byte.astype(np.uint8).reshape(k // 512, 16, n))


def unpack_weight(words, scales, fmt):
    g, _, n = scales.shape
    words = np.ascontiguousarray(words).reshape(g, 128, n, -1)
    if fmt == "e4m3":
        vals = words.view(ml_dtypes.float8_e4m3fn).astype(np.float64)
    else:
        nib = np.empty((g, 128, n, 4), np.uint8)
        nib[..., 0::2] = words & 0xF
        nib[..., 1::2] = words >> 4
        vals = E2M1[nib]
    vals = vals * np.repeat(np.exp2(scales.astype(np.float64) - 127.0), 8, axis=1)[..., None]
    return vals.transpose(0, 1, 3, 2).reshape(g * 512, n)


def sigmoid(v):
    return 1.0 / (1.0 + np.exp(-v))


D, T, I, Q = 512, 1024, 512, 128


def setup_inputs():
    n = np.random.standard_normal
    idx = np.stack([np.random.permutation(T)[:I] for _ in range(8)])
    idx2 = np.stack([np.random.permutation(T)[:I] for _ in range(8)])
    idx3 = np.stack([np.random.permutation(T)[:I] for _ in range(8)])
    fd = mx_kscale(D)
    keysp = pack_weight(n((D, T)) / fd[:, None], "e2m1")
    return {
        "query": (n((D, Q)) * 1.0 / np.sqrt(D) * fd[:, None]).astype(np.float32),
        "keys_words": keysp[0],
        "keys_scales": keysp[1],
        "lam": (np.random.uniform(0.3, 0.9, (Q, 1))).astype(np.float32),
        "eager": (np.random.uniform(0.8, 2.0, (Q, 1))).astype(np.float32),
        "thresh": (np.random.uniform(1.5, 4.0, (Q, 1))).astype(np.float32),
        "base": (0.3 * n((Q, I))).astype(np.float32),
        "gain2": (np.random.uniform(0.5, 2.0, (Q, 1))).astype(np.float32),
        "offs": striped8(idx),
        "offs2": striped8(idx2),
        "offs3": striped8(idx3),
    }


def reference(query, keys_words, keys_scales, lam, eager, thresh, base, gain2, offs, offs2, offs3):
    idx = unstriped8(offs)
    idx2 = unstriped8(offs2)
    idx3 = unstriped8(offs3)
    keysu = unpack_weight(keys_words, keys_scales, "e2m1")
    queryq = mxq(f64(query), 0, "e4m3")
    a = queryq.T @ keysu
    rv = np.log(np.exp(pick8(a, idx2, 16)) + np.exp(pick8(a, idx3, 16)))
    s = pick8(a, idx, 16) - rv * f64(lam)
    m0 = np.max(s, axis=1, keepdims=True)
    m1 = np.mean(s, axis=1, keepdims=True)
    p = np.exp(s - m0)
    gt0 = sigmoid((m0 - m1) * f64(eager) - f64(thresh))
    w = p / np.sum(p, axis=1, keepdims=True) * gt0
    y = np.tanh(w * f64(gain2) * 256.0) + f64(base)
    return y

@@ -1,0 +1,171 @@
+from contextlib import ExitStack
+
+import concourse.mybir as mybir
+
+D, T, I, Q = 512, 1024, 512, 128
+FLOPS = 2 * D * T * Q
+
+F32 = mybir.dt.float32
+BF16 = mybir.dt.bfloat16
+I32 = mybir.dt.int32
+U32 = mybir.dt.uint32
+U16 = mybir.dt.uint16
+U8 = mybir.dt.uint8
+FP8X4 = mybir.dt.float8_e4m3fn_x4
+FP4X4 = mybir.dt.float4_e2m1fn_x4
+ALU = mybir.AluOpType
+ACT = mybir.ActivationFunctionType
+AXIS = mybir.AxisListType
+
+P = 128
+PACK = 4
+N_PASS = 256
+HALF = I // 2
+LIST_COLS = I // 16
+
+
+def tile_attend_tworivals_abstaining_gated_heads_kernel(
+    tc, query, keys_words, keys_scales, lam, eager, thresh, base, gain2, offs, offs2, offs3, out
+):
+    nc = tc.nc
+    with ExitStack() as ctx:
+        held = ctx.enter_context(tc.tile_pool(name="held", bufs=1))
+        psum = ctx.enter_context(tc.psum_pool(name="psum", bufs=1))
+
+        def column(name):
+            return held.tile([P, 1], F32, name=name)
+
+        def slots(name):
+            return held.tile([P, I], F32, name=name)
+
+        q_raw = held.tile([P, PACK, Q], F32)
+        nc.sync.dma_start(out=q_raw[:], in_=query.rearrange("(p j) q -> p j q", j=PACK))
+        k_words = held.tile([P, 2 * T], U8, align_bytes=64)
+        nc.sync.dma_start(out=k_words[:].bitcast(I32), in_=keys_words[0].bitcast(I32))
+        k_scales = held.tile([P, T], U8, align_bytes=64)
+        nc.gpsimd.memset(k_scales[:].bitcast(I32), 0)
+        for quad in range(4):
+            nc.scalar.dma_start(
+                out=k_scales[32 * quad : 32 * quad + 4, :].bitcast(I32),
+                in_=keys_scales[0, 4 * quad : 4 * quad + 4, :].bitcast(I32),
+            )
+        list_rival2 = held.tile([P, LIST_COLS], U16)
+        nc.sync.dma_start(list_rival2[:], offs2)
+        list_rival3 = held.tile([P, LIST_COLS], U16)
+        nc.sync.dma_start(list_rival3[:], offs3)
+        list_token = held.tile([P, LIST_COLS], U16)
+        nc.sync.dma_start(list_token[:], offs)
+        lam_col = column("lam_col")
+        nc.sync.dma_start(out=lam_col[:], in_=lam)
+        eager_col = column("eager_col")
+        nc.sync.dma_start(out=eager_col[:], in_=eager)
+        thresh_col = column("thresh_col")
+        nc.sync.dma_start(out=thresh_col[:], in_=thresh)
+        gain_col = column("gain_col")
+        nc.sync.dma_start(out=gain_col[:], in_=gain2)
+        base_sb = slots("base_sb")
+        nc.sync.dma_start(out=base_sb[:], in_=base)
+
+        q_grouped = held.tile([P, Q * PACK], BF16, align_bytes=64)
+        nc.vector.tensor_copy(
+            out=q_grouped[:].rearrange("p (c i t) -> p c t i", i=4, t=PACK),
+            in_=q_raw[:].rearrange("p t (c i) -> p c t i", i=4),
+        )
+        q_codes = held.tile([P, Q], U32, align_bytes=64)
+        q_scales = held.tile([P, Q], U8, align_bytes=64)
+        nc.vector.quantize_mx(out=q_codes[:].bitcast(FP8X4), scales=q_scales[:], in_=q_grouped[:])
+
+        a_sb = held.tile([P, T], F32)
+        for n in range(T // N_PASS):
+            cols = slice(n * N_PASS, (n + 1) * N_PASS)
+            bank = psum.tile([P, N_PASS], F32, name="bank%d" % n)
+            nc.tensor.matmul_mx(
+                out=bank[:],
+                lhsT=q_codes[:].bitcast(FP8X4),
+                lhsT_scale=q_scales[:],
+                rhs=k_words[:, 2 * cols.start : 2 * cols.stop].bitcast(FP4X4),
+                rhs_scale=k_scales[:, cols],
+                start=True,
+                stop=True,
+            )
+            if n % 2 == 0:
+                nc.scalar.activation(out=a_sb[:, cols], in_=bank[:], func=ACT.Copy)
+            else:
+                nc.vector.tensor_copy(out=a_sb[:, cols], in_=bank[:])
+
+        def looked_up(offsets, half):
+            return a_sb[:].indirect(offsets[:, half * LIST_COLS // 2 : (half + 1) * LIST_COLS // 2])
+
+        first, second = slice(0, HALF), slice(HALF, I)
+        rival2 = slots("rival2")
+        diff = slots("diff")
+        rival3_second = held.tile([P, HALF], F32)
+        nc.scalar.activation(out=rival2[:, first], in_=looked_up(list_rival2, 0), func=ACT.Copy)
+        nc.vector.tensor_copy(out=rival2[:, second], in_=looked_up(list_rival2, 1))
+        nc.scalar.activation(out=rival3_second[:], in_=looked_up(list_rival3, 1), func=ACT.Copy)
+        nc.vector.tensor_tensor(diff[:, first], looked_up(list_rival3, 0), rival2[:, first], ALU.subtract)
+        nc.vector.tensor_tensor(diff[:, second], rival3_second[:], rival2[:, second], ALU.subtract)
+
+        gap = slots("gap")
+        small = slots("small")
+        nc.scalar.activation(out=gap[:, first], in_=diff[:, first], func=ACT.Abs)
+        nc.scalar.activation(out=small[:, first], in_=gap[:, first], func=ACT.Exp, scale=-1.0)
+        nc.vector.scalar_tensor_tensor(
+            out=gap[:, second], in0=diff[:, second], scalar=-1.0, in1=diff[:, second], op0=ALU.mult, op1=ALU.max
+        )
+        nc.scalar.activation(out=small[:, second], in_=gap[:, second], func=ACT.Exp, scale=-1.0)
+        log_rest = slots("log_rest")
+        nc.scalar.activation(out=log_rest[:], in_=small[:], func=ACT.Ln, bias=1.0)
+
+        larger = slots("larger")
+        nc.vector.scalar_tensor_tensor(
+            out=larger[:], in0=diff[:], scalar=0.0, in1=rival2[:], op0=ALU.max, op1=ALU.add
+        )
+        lam_larger = slots("lam_larger")
+        nc.vector.tensor_scalar(out=lam_larger[:], in0=larger[:], scalar1=lam_col[:], scalar2=None, op0=ALU.mult)
+        partial = slots("partial")
+        nc.vector.tensor_tensor(partial[:], a_sb[:].indirect(list_token[:]), lam_larger[:], ALU.subtract)
+
+        neg_lam = column("neg_lam")
+        nc.vector.tensor_scalar(out=neg_lam[:], in0=lam_col[:], scalar1=-1.0, scalar2=None, op0=ALU.mult)
+        gate_scale = column("gate_scale")
+        nc.vector.tensor_scalar(out=gate_scale[:], in0=eager_col[:], scalar1=-0.5, scalar2=None, op0=ALU.mult)
+        gate_bias = column("gate_bias")
+        nc.vector.tensor_scalar(out=gate_bias[:], in0=thresh_col[:], scalar1=-0.5, scalar2=None, op0=ALU.mult)
+        half_gain = column("half_gain")
+        nc.vector.tensor_scalar(out=half_gain[:], in0=gain_col[:], scalar1=128.0, scalar2=None, op0=ALU.mult)
+
+        score = slots("score")
+        score_sum = column("score_sum")
+        nc.vector.scalar_tensor_tensor(
+            out=score[:], in0=log_rest[:], scalar=neg_lam[:], in1=partial[:], op0=ALU.mult, op1=ALU.add,
+            accum_out=score_sum[:],
+        )
+        neg_max = column("neg_max")
+        nc.vector.tensor_reduce(out=neg_max[:], in_=score[:], axis=AXIS.X, op=ALU.max, negate=True)
+        mean_less_max = column("mean_less_max")
+        nc.vector.scalar_tensor_tensor(
+            out=mean_less_max[:], in0=score_sum[:], scalar=1.0 / I, in1=neg_max[:], op0=ALU.mult, op1=ALU.add
+        )
+        gate_tanh = column("gate_tanh")
+        nc.scalar.activation(
+            out=gate_tanh[:], in_=mean_less_max[:], func=ACT.Tanh, scale=gate_scale[:], bias=gate_bias[:]
+        )
+        share = slots("share")
+        share_sum = column("share_sum")
+        nc.scalar.activation(out=share[:], in_=score[:], func=ACT.Exp, bias=neg_max[:], accum_out=share_sum[:])
+        gated_gain = column("gated_gain")
+        nc.vector.tensor_scalar(
+            out=gated_gain[:], in0=gate_tanh[:], scalar1=1.0, scalar2=half_gain[:], op0=ALU.add, op1=ALU.mult
+        )
+        inv_sum = column("inv_sum")
+        nc.vector.reciprocal(out=inv_sum[:], in_=share_sum[:])
+        row_factor = column("row_factor")
+        nc.vector.tensor_tensor(row_factor[:], inv_sum[:], gated_gain[:], ALU.mult)
+
+        squashed = slots("squashed")
+        result = slots("result")
+        for cols in (first, second):
+            nc.scalar.activation(out=squashed[:, cols], in_=share[:, cols], func=ACT.Tanh, scale=row_factor[:])
+            nc.vector.tensor_tensor(result[:, cols], squashed[:, cols], base_sb[:, cols], ALU.add)
+            nc.sync.dma_start(out=out[:, cols], in_=result[:, cols])

@@ -1,3 +1,4 @@
+import math
 from contextlib import ExitStack
 
 import concourse.mybir as mybir
@@ -19,7 +20,11 @@ AXIS = mybir.AxisListType
 
 P = 128
 PACK = 4
-N_PASS = 256
+PASS_WIDTHS = (256, 256, 256, 128, 128)
+SCALAR_PASSES = (0, 2)
+OUT_WIDTHS = (192, 192, 128)
+EXP_CAP = 2.0**30
+DIFF_CAP = 30 * math.log(2.0)
 HALF = I // 2
 LIST_COLS = I // 16
 
@@ -40,15 +45,14 @@ def tile_attend_tworivals_abstaining_gated_heads_kernel(
 
         q_raw = held.tile([P, PACK, Q], F32)
         nc.sync.dma_start(out=q_raw[:], in_=query.rearrange("(p j) q -> p j q", j=PACK))
-        k_words = held.tile([P, 2 * T], U8, align_bytes=64)
-        nc.sync.dma_start(out=k_words[:].bitcast(I32), in_=keys_words[0].bitcast(I32))
         k_scales = held.tile([P, T], U8, align_bytes=64)
-        nc.gpsimd.memset(k_scales[:].bitcast(I32), 0)
         for quad in range(4):
-            nc.scalar.dma_start(
+            nc.sync.dma_start(
                 out=k_scales[32 * quad : 32 * quad + 4, :].bitcast(I32),
                 in_=keys_scales[0, 4 * quad : 4 * quad + 4, :].bitcast(I32),
             )
+        k_words = held.tile([P, 2 * T], U8, align_bytes=64)
+        nc.sync.dma_start(out=k_words[:].bitcast(I32), in_=keys_words[0].bitcast(I32))
         list_rival2 = held.tile([P, LIST_COLS], U16)
         nc.sync.dma_start(list_rival2[:], offs2)
         list_rival3 = held.tile([P, LIST_COLS], U16)
@@ -67,18 +71,27 @@ def tile_attend_tworivals_abstaining_gated_heads_kernel(
         nc.sync.dma_start(out=base_sb[:], in_=base)
 
         q_grouped = held.tile([P, Q * PACK], BF16, align_bytes=64)
-        nc.vector.tensor_copy(
-            out=q_grouped[:].rearrange("p (c i t) -> p c t i", i=4, t=PACK),
-            in_=q_raw[:].rearrange("p t (c i) -> p c t i", i=4),
-        )
         q_codes = held.tile([P, Q], U32, align_bytes=64)
         q_scales = held.tile([P, Q], U8, align_bytes=64)
-        nc.vector.quantize_mx(out=q_codes[:].bitcast(FP8X4), scales=q_scales[:], in_=q_grouped[:])
+        row_halves = (slice(0, Q // 2), slice(Q // 2, Q))
+        for rows in row_halves:
+            nc.vector.tensor_copy(
+                out=q_grouped[:, PACK * rows.start : PACK * rows.stop].rearrange("p (c i t) -> p c t i", i=4, t=PACK),
+                in_=q_raw[:, :, rows].rearrange("p t (c i) -> p c t i", i=4),
+            )
+        for rows in row_halves:
+            nc.vector.quantize_mx(
+                out=q_codes[:, rows].bitcast(FP8X4),
+                scales=q_scales[:, rows],
+                in_=q_grouped[:, PACK * rows.start : PACK * rows.stop],
+            )
 
         a_sb = held.tile([P, T], F32)
-        for n in range(T // N_PASS):
-            cols = slice(n * N_PASS, (n + 1) * N_PASS)
-            bank = psum.tile([P, N_PASS], F32, name="bank%d" % n)
+        start = 0
+        for n, width in enumerate(PASS_WIDTHS):
+            cols = slice(start, start + width)
+            start = cols.stop
+            bank = psum.tile([P, width], F32, name="bank%d" % n)
             nc.tensor.matmul_mx(
                 out=bank[:],
                 lhsT=q_codes[:].bitcast(FP8X4),
@@ -88,7 +101,7 @@ def tile_attend_tworivals_abstaining_gated_heads_kernel(
                 start=True,
                 stop=True,
             )
-            if n % 2 == 0:
+            if n in SCALAR_PASSES:
                 nc.scalar.activation(out=a_sb[:, cols], in_=bank[:], func=ACT.Copy)
             else:
                 nc.vector.tensor_copy(out=a_sb[:, cols], in_=bank[:])
@@ -99,73 +112,80 @@ def tile_attend_tworivals_abstaining_gated_heads_kernel(
         first, second = slice(0, HALF), slice(HALF, I)
         rival2 = slots("rival2")
         diff = slots("diff")
-        rival3_second = held.tile([P, HALF], F32)
+        token = slots("token")
+        rival3_second = token[:, second]
         nc.scalar.activation(out=rival2[:, first], in_=looked_up(list_rival2, 0), func=ACT.Copy)
         nc.vector.tensor_copy(out=rival2[:, second], in_=looked_up(list_rival2, 1))
-        nc.scalar.activation(out=rival3_second[:], in_=looked_up(list_rival3, 1), func=ACT.Copy)
+        nc.scalar.activation(out=rival3_second, in_=looked_up(list_rival3, 1), func=ACT.Copy)
         nc.vector.tensor_tensor(diff[:, first], looked_up(list_rival3, 0), rival2[:, first], ALU.subtract)
-        nc.vector.tensor_tensor(diff[:, second], rival3_second[:], rival2[:, second], ALU.subtract)
+        nc.vector.tensor_tensor(diff[:, second], rival3_second, rival2[:, second], ALU.subtract)
 
-        gap = slots("gap")
-        small = slots("small")
-        nc.scalar.activation(out=gap[:, first], in_=diff[:, first], func=ACT.Abs)
-        nc.scalar.activation(out=small[:, first], in_=gap[:, first], func=ACT.Exp, scale=-1.0)
-        nc.vector.scalar_tensor_tensor(
-            out=gap[:, second], in0=diff[:, second], scalar=-1.0, in1=diff[:, second], op0=ALU.mult, op1=ALU.max
-        )
-        nc.scalar.activation(out=small[:, second], in_=gap[:, second], func=ACT.Exp, scale=-1.0)
-        log_rest = slots("log_rest")
-        nc.scalar.activation(out=log_rest[:], in_=small[:], func=ACT.Ln, bias=1.0)
+        ratio = slots("ratio")
+        for cols in (first, second):
+            nc.scalar.activation(out=ratio[:, cols], in_=diff[:, cols], func=ACT.Exp)
+        lifted = slots("lifted")
 
-        larger = slots("larger")
-        nc.vector.scalar_tensor_tensor(
-            out=larger[:], in0=diff[:], scalar=0.0, in1=rival2[:], op0=ALU.max, op1=ALU.add
-        )
-        lam_larger = slots("lam_larger")
-        nc.vector.tensor_scalar(out=lam_larger[:], in0=larger[:], scalar1=lam_col[:], scalar2=None, op0=ALU.mult)
-        partial = slots("partial")
-        nc.vector.tensor_tensor(partial[:], a_sb[:].indirect(list_token[:]), lam_larger[:], ALU.subtract)
+        def lift(cols):
+            nc.vector.scalar_tensor_tensor(
+                out=lifted[:, cols], in0=diff[:, cols], scalar=DIFF_CAP, in1=rival2[:, cols], op0=ALU.max, op1=ALU.add
+            )
 
-        neg_lam = column("neg_lam")
-        nc.vector.tensor_scalar(out=neg_lam[:], in0=lam_col[:], scalar1=-1.0, scalar2=None, op0=ALU.mult)
-        gate_scale = column("gate_scale")
-        nc.vector.tensor_scalar(out=gate_scale[:], in0=eager_col[:], scalar1=-0.5, scalar2=None, op0=ALU.mult)
-        gate_bias = column("gate_bias")
-        nc.vector.tensor_scalar(out=gate_bias[:], in0=thresh_col[:], scalar1=-0.5, scalar2=None, op0=ALU.mult)
-        half_gain = column("half_gain")
-        nc.vector.tensor_scalar(out=half_gain[:], in0=gain_col[:], scalar1=128.0, scalar2=None, op0=ALU.mult)
+        lift(first)
+        nc.vector.tensor_copy(out=token[:], in_=a_sb[:].indirect(list_token[:]))
+        lift(second)
+        capped = slots("capped")
+        nc.vector.tensor_scalar(out=capped[:], in0=ratio[:], scalar1=EXP_CAP, scalar2=None, op0=ALU.min)
+        neg_partial = slots("neg_partial")
+        for cols in (first, second):
+            nc.vector.scalar_tensor_tensor(
+                out=neg_partial[:, cols], in0=lifted[:, cols], scalar=lam_col[:], in1=token[:, cols],
+                op0=ALU.mult, op1=ALU.subtract,
+            )
 
-        score = slots("score")
-        score_sum = column("score_sum")
-        nc.vector.scalar_tensor_tensor(
-            out=score[:], in0=log_rest[:], scalar=neg_lam[:], in1=partial[:], op0=ALU.mult, op1=ALU.add,
-            accum_out=score_sum[:],
-        )
+        log_part = slots("log_part")
+        neg_score = slots("neg_score")
+        half_sums = held.tile([P, 2], F32)
+        for cols in (first, second):
+            nc.scalar.activation(out=log_part[:, cols], in_=capped[:, cols], func=ACT.Ln, bias=1.0)
+        for h, cols in enumerate((first, second)):
+            nc.vector.scalar_tensor_tensor(
+                out=neg_score[:, cols], in0=log_part[:, cols], scalar=lam_col[:], in1=neg_partial[:, cols],
+                op0=ALU.mult, op1=ALU.add, accum_out=half_sums[:, h : h + 1],
+            )
         neg_max = column("neg_max")
-        nc.vector.tensor_reduce(out=neg_max[:], in_=score[:], axis=AXIS.X, op=ALU.max, negate=True)
-        mean_less_max = column("mean_less_max")
-        nc.vector.scalar_tensor_tensor(
-            out=mean_less_max[:], in0=score_sum[:], scalar=1.0 / I, in1=neg_max[:], op0=ALU.mult, op1=ALU.add
-        )
-        gate_tanh = column("gate_tanh")
-        nc.scalar.activation(
-            out=gate_tanh[:], in_=mean_less_max[:], func=ACT.Tanh, scale=gate_scale[:], bias=gate_bias[:]
-        )
+        nc.vector.tensor_reduce(out=neg_max[:], in_=neg_score[:], axis=AXIS.X, op=ALU.min)
         share = slots("share")
         share_sum = column("share_sum")
-        nc.scalar.activation(out=share[:], in_=score[:], func=ACT.Exp, bias=neg_max[:], accum_out=share_sum[:])
-        gated_gain = column("gated_gain")
-        nc.vector.tensor_scalar(
-            out=gated_gain[:], in0=gate_tanh[:], scalar1=1.0, scalar2=half_gain[:], op0=ALU.add, op1=ALU.mult
+        nc.scalar.activation(
+            out=share[:], in_=neg_score[:], func=ACT.Exp, scale=-1.0, bias=neg_max[:], accum_out=share_sum[:]
         )
-        inv_sum = column("inv_sum")
-        nc.vector.reciprocal(out=inv_sum[:], in_=share_sum[:])
+        half_means = held.tile([P, 2], F32)
+        mean_less_max = column("mean_less_max")
+        nc.vector.tensor_scalar(
+            out=half_means[:], in0=half_sums[:], scalar1=-1.0 / I, scalar2=neg_max[:], op0=ALU.mult, op1=ALU.add,
+            accum_out=mean_less_max[:],
+        )
+        odds = column("odds")
+        nc.scalar.activation(out=odds[:], in_=mean_less_max[:], func=ACT.Exp, scale=eager_col[:], bias=thresh_col[:])
+        denominator = column("denominator")
+        nc.vector.tensor_scalar(
+            out=denominator[:], in0=odds[:], scalar1=1.0, scalar2=share_sum[:], op0=ALU.add, op1=ALU.mult
+        )
         row_factor = column("row_factor")
-        nc.vector.tensor_tensor(row_factor[:], inv_sum[:], gated_gain[:], ALU.mult)
+        nc.vector.reciprocal(out=row_factor[:], in_=denominator[:])
 
+        gained = slots("gained")
         squashed = slots("squashed")
         result = slots("result")
         for cols in (first, second):
-            nc.scalar.activation(out=squashed[:, cols], in_=share[:, cols], func=ACT.Tanh, scale=row_factor[:])
+            nc.vector.tensor_scalar(
+                out=gained[:, cols], in0=share[:, cols], scalar1=gain_col[:], scalar2=256.0,
+                op0=ALU.mult, op1=ALU.mult,
+            )
+        start = 0
+        for width in OUT_WIDTHS:
+            cols = slice(start, start + width)
+            start = cols.stop
+            nc.scalar.activation(out=squashed[:, cols], in_=gained[:, cols], func=ACT.Tanh, scale=row_factor[:])
             nc.vector.tensor_tensor(result[:, cols], squashed[:, cols], base_sb[:, cols], ALU.add)
             nc.sync.dma_start(out=out[:, cols], in_=result[:, cols])

import math
from contextlib import ExitStack

import concourse.mybir as mybir

D, T, I, Q = 512, 1024, 512, 128
FLOPS = 2 * D * T * Q

F32 = mybir.dt.float32
BF16 = mybir.dt.bfloat16
I32 = mybir.dt.int32
U32 = mybir.dt.uint32
U16 = mybir.dt.uint16
U8 = mybir.dt.uint8
FP8X4 = mybir.dt.float8_e4m3fn_x4
FP4X4 = mybir.dt.float4_e2m1fn_x4
ALU = mybir.AluOpType
ACT = mybir.ActivationFunctionType
AXIS = mybir.AxisListType

P = 128
PACK = 4
PASS_WIDTHS = (256, 256, 256, 128, 128)
SCALAR_PASSES = (0, 2)
OUT_WIDTHS = (192, 192, 128)
EXP_CAP = 2.0**30
DIFF_CAP = 30 * math.log(2.0)
HALF = I // 2
LIST_COLS = I // 16


def tile_attend_tworivals_abstaining_gated_heads_kernel(
    tc, query, keys_words, keys_scales, lam, eager, thresh, base, gain2, offs, offs2, offs3, out
):
    nc = tc.nc
    with ExitStack() as ctx:
        held = ctx.enter_context(tc.tile_pool(name="held", bufs=1))
        psum = ctx.enter_context(tc.psum_pool(name="psum", bufs=1))

        def column(name):
            return held.tile([P, 1], F32, name=name)

        def slots(name):
            return held.tile([P, I], F32, name=name)

        q_raw = held.tile([P, PACK, Q], F32)
        nc.sync.dma_start(out=q_raw[:], in_=query.rearrange("(p j) q -> p j q", j=PACK))
        k_scales = held.tile([P, T], U8, align_bytes=64)
        for quad in range(4):
            nc.sync.dma_start(
                out=k_scales[32 * quad : 32 * quad + 4, :].bitcast(I32),
                in_=keys_scales[0, 4 * quad : 4 * quad + 4, :].bitcast(I32),
            )
        k_words = held.tile([P, 2 * T], U8, align_bytes=64)
        nc.sync.dma_start(out=k_words[:].bitcast(I32), in_=keys_words[0].bitcast(I32))
        list_rival2 = held.tile([P, LIST_COLS], U16)
        nc.sync.dma_start(list_rival2[:], offs2)
        list_rival3 = held.tile([P, LIST_COLS], U16)
        nc.sync.dma_start(list_rival3[:], offs3)
        list_token = held.tile([P, LIST_COLS], U16)
        nc.sync.dma_start(list_token[:], offs)
        lam_col = column("lam_col")
        nc.sync.dma_start(out=lam_col[:], in_=lam)
        eager_col = column("eager_col")
        nc.sync.dma_start(out=eager_col[:], in_=eager)
        thresh_col = column("thresh_col")
        nc.sync.dma_start(out=thresh_col[:], in_=thresh)
        gain_col = column("gain_col")
        nc.sync.dma_start(out=gain_col[:], in_=gain2)
        base_sb = slots("base_sb")
        nc.sync.dma_start(out=base_sb[:], in_=base)

        q_grouped = held.tile([P, Q * PACK], BF16, align_bytes=64)
        q_codes = held.tile([P, Q], U32, align_bytes=64)
        q_scales = held.tile([P, Q], U8, align_bytes=64)
        row_halves = (slice(0, Q // 2), slice(Q // 2, Q))
        for rows in row_halves:
            nc.vector.tensor_copy(
                out=q_grouped[:, PACK * rows.start : PACK * rows.stop].rearrange("p (c i t) -> p c t i", i=4, t=PACK),
                in_=q_raw[:, :, rows].rearrange("p t (c i) -> p c t i", i=4),
            )
        for rows in row_halves:
            nc.vector.quantize_mx(
                out=q_codes[:, rows].bitcast(FP8X4),
                scales=q_scales[:, rows],
                in_=q_grouped[:, PACK * rows.start : PACK * rows.stop],
            )

        a_sb = held.tile([P, T], F32)
        start = 0
        for n, width in enumerate(PASS_WIDTHS):
            cols = slice(start, start + width)
            start = cols.stop
            bank = psum.tile([P, width], F32, name="bank%d" % n)
            nc.tensor.matmul_mx(
                out=bank[:],
                lhsT=q_codes[:].bitcast(FP8X4),
                lhsT_scale=q_scales[:],
                rhs=k_words[:, 2 * cols.start : 2 * cols.stop].bitcast(FP4X4),
                rhs_scale=k_scales[:, cols],
                start=True,
                stop=True,
            )
            if n in SCALAR_PASSES:
                nc.scalar.activation(out=a_sb[:, cols], in_=bank[:], func=ACT.Copy)
            else:
                nc.vector.tensor_copy(out=a_sb[:, cols], in_=bank[:])

        def looked_up(offsets, half):
            return a_sb[:].indirect(offsets[:, half * LIST_COLS // 2 : (half + 1) * LIST_COLS // 2])

        first, second = slice(0, HALF), slice(HALF, I)
        rival2 = slots("rival2")
        diff = slots("diff")
        token = slots("token")
        rival3_second = token[:, second]
        nc.scalar.activation(out=rival2[:, first], in_=looked_up(list_rival2, 0), func=ACT.Copy)
        nc.vector.tensor_copy(out=rival2[:, second], in_=looked_up(list_rival2, 1))
        nc.scalar.activation(out=rival3_second, in_=looked_up(list_rival3, 1), func=ACT.Copy)
        nc.vector.tensor_tensor(diff[:, first], looked_up(list_rival3, 0), rival2[:, first], ALU.subtract)
        nc.vector.tensor_tensor(diff[:, second], rival3_second, rival2[:, second], ALU.subtract)

        ratio = slots("ratio")
        for cols in (first, second):
            nc.scalar.activation(out=ratio[:, cols], in_=diff[:, cols], func=ACT.Exp)
        lifted = slots("lifted")

        def lift(cols):
            nc.vector.scalar_tensor_tensor(
                out=lifted[:, cols], in0=diff[:, cols], scalar=DIFF_CAP, in1=rival2[:, cols], op0=ALU.max, op1=ALU.add
            )

        lift(first)
        nc.vector.tensor_copy(out=token[:], in_=a_sb[:].indirect(list_token[:]))
        lift(second)
        capped = slots("capped")
        nc.vector.tensor_scalar(out=capped[:], in0=ratio[:], scalar1=EXP_CAP, scalar2=None, op0=ALU.min)
        neg_partial = slots("neg_partial")
        for cols in (first, second):
            nc.vector.scalar_tensor_tensor(
                out=neg_partial[:, cols], in0=lifted[:, cols], scalar=lam_col[:], in1=token[:, cols],
                op0=ALU.mult, op1=ALU.subtract,
            )

        log_part = slots("log_part")
        neg_score = slots("neg_score")
        half_sums = held.tile([P, 2], F32)
        for cols in (first, second):
            nc.scalar.activation(out=log_part[:, cols], in_=capped[:, cols], func=ACT.Ln, bias=1.0)
        for h, cols in enumerate((first, second)):
            nc.vector.scalar_tensor_tensor(
                out=neg_score[:, cols], in0=log_part[:, cols], scalar=lam_col[:], in1=neg_partial[:, cols],
                op0=ALU.mult, op1=ALU.add, accum_out=half_sums[:, h : h + 1],
            )
        neg_max = column("neg_max")
        nc.vector.tensor_reduce(out=neg_max[:], in_=neg_score[:], axis=AXIS.X, op=ALU.min)
        share = slots("share")
        share_sum = column("share_sum")
        nc.scalar.activation(
            out=share[:], in_=neg_score[:], func=ACT.Exp, scale=-1.0, bias=neg_max[:], accum_out=share_sum[:]
        )
        half_means = held.tile([P, 2], F32)
        mean_less_max = column("mean_less_max")
        nc.vector.tensor_scalar(
            out=half_means[:], in0=half_sums[:], scalar1=-1.0 / I, scalar2=neg_max[:], op0=ALU.mult, op1=ALU.add,
            accum_out=mean_less_max[:],
        )
        odds = column("odds")
        nc.scalar.activation(out=odds[:], in_=mean_less_max[:], func=ACT.Exp, scale=eager_col[:], bias=thresh_col[:])
        denominator = column("denominator")
        nc.vector.tensor_scalar(
            out=denominator[:], in0=odds[:], scalar1=1.0, scalar2=share_sum[:], op0=ALU.add, op1=ALU.mult
        )
        row_factor = column("row_factor")
        nc.vector.reciprocal(out=row_factor[:], in_=denominator[:])

        gained = slots("gained")
        squashed = slots("squashed")
        result = slots("result")
        for cols in (first, second):
            nc.vector.tensor_scalar(
                out=gained[:, cols], in0=share[:, cols], scalar1=gain_col[:], scalar2=256.0,
                op0=ALU.mult, op1=ALU.mult,
            )
        start = 0
        for width in OUT_WIDTHS:
            cols = slice(start, start + width)
            start = cols.stop
            nc.scalar.activation(out=squashed[:, cols], in_=gained[:, cols], func=ACT.Tanh, scale=row_factor[:])
            nc.vector.tensor_tensor(result[:, cols], squashed[:, cols], base_sb[:, cols], ALU.add)
            nc.sync.dma_start(out=out[:, cols], in_=result[:, cols])
